import numpy as np
import ml_dtypes


def mxq(x, axis, fmt="e4m3"):
    dtype, down = {"e4m3": (ml_dtypes.float8_e4m3fn, 7), "e5m2": (ml_dtypes.float8_e5m2, 14)}[fmt]
    v = np.moveaxis(np.asarray(x, np.float32).astype(ml_dtypes.bfloat16).astype(np.float64), axis, -1)
    blocks = v.reshape(v.shape[:-1] + (-1, 32))
    amax = np.abs(blocks).max(-1, keepdims=True)
    byte = np.maximum(np.where(amax > 0, np.frexp(amax)[1] - 1 + 127, 0) - down, 1)
    scale = np.exp2(byte - 127.0)
    codes = (blocks / scale).astype(np.float32).astype(dtype).astype(np.float64)
    return np.moveaxis((codes * scale).reshape(v.shape), -1, axis)


WIDE = False


def mx_kscale(k):
    if not WIDE:
        return np.ones(k)
    levels = np.array([30, -30])
    if k % 512:
        return np.exp2(np.random.permutation(np.resize(levels, k // 32))).repeat(32)
    a = np.empty((k // 512, 16))
    for p in range(k // 512):
        a[p, :8] = np.random.permutation(np.resize(levels, 8))
        for g in range(8):
            far = levels[np.abs(levels - a[p, g]) >= 10]
            a[p, g + 8] = far[np.random.randint(len(far))]
    return np.exp2(a.ravel()).repeat(32)


def f64(x):
    return np.asarray(x).astype(np.float64)


def striped(idx):
    return np.tile(np.asarray(idx).reshape(-1, 16).T, (8, 1)).astype(np.uint16)


def unstriped(offs):
    return offs[:16].T.reshape(-1).astype(np.int64)


E2M1 = np.array([0.0, 0.5, 1.0, 1.5, 2.0, 3.0, 4.0, 6.0, -0.0, -0.5, -1.0, -1.5, -2.0, -3.0, -4.0, -6.0])


def pack_weight(w, fmt):
    k, n = w.shape
    w = f64(np.asarray(w, np.float32).astype(ml_dtypes.bfloat16)).reshape(k // 32, 32, n)
    amax = np.abs(w).max(1)
    if fmt == "e4m3":
        byte = np.frexp(amax)[1] - 1 + 127 - 7
    else:
        mant, ex = np.frexp(amax / 6.0)
        byte = np.where(mant > 0.5, ex, ex - 1) + 127
    byte = np.clip(np.where(amax > 0, byte, 1), 1, 254)
    scaled = (w * np.exp2(127.0 - byte)[:, None, :]).reshape(k, n).astype(np.float32)
    by_word = np.ascontiguousarray(scaled.reshape(k // 512, 128, 4, n).transpose(0, 1, 3, 2))
    if fmt == "e4m3":
        words = by_word.astype(ml_dtypes.float8_e4m3fn).view(np.uint8)
    else:
        c = by_word.astype(ml_dtypes.float4_e2m1fn).view(np.uint8) & 0xF
        words = (c[..., 0::2] | (c[..., 1::2] << 4)).reshape(k // 512, 128, 2 * n)
    return np.ascontiguousarray(words), np.ascontiguousarray(byte.astype(np.uint8).reshape(k // 512, 16, n))


def unpack_weight(words, scales, fmt):
    g, _, n = scales.shape
    words = np.ascontiguousarray(words).reshape(g, 128, n, -1)
    if fmt == "e4m3":
        vals = words.view(ml_dtypes.float8_e4m3fn).astype(np.float64)
    else:
        nib = np.empty((g, 128, n, 4), np.uint8)
        nib[..., 0::2] = words & 0xF
        nib[..., 1::2] = words >> 4
        vals = E2M1[nib]
    vals = vals * np.repeat(np.exp2(scales.astype(np.float64) - 127.0), 8, axis=1)[..., None]
    return vals.transpose(0, 1, 3, 2).reshape(g * 512, n)


K, R, N, T, J, B = 512, 512, 512, 1024, 512, 128


def setup_inputs():
    n = np.random.standard_normal
    idx = np.random.permutation(T)[:J]
    fn = mx_kscale(N)
    fr = mx_kscale(R)
    wdp = pack_weight(n((N, R)) * 1 / np.sqrt(N) * fn[:, None], "e2m1")
    wup = pack_weight(n((R, K)) * 1 / np.sqrt(R) / fr[:, None], "e4m3")
    return {
        "g": (n((N, T)) * np.exp(0.5 * n((1, T))) / fn[:, None]).astype(np.float32),
        "wd_words": wdp[0],
        "wd_scales": wdp[1],
        "us": (np.random.uniform(0.5, 2.0, (R, 1)) * fr[:, None]).astype(np.float32),
        "wu_words": wup[0],
        "wu_scales": wup[1],
        "offs": striped(idx),
    }


def reference(g, wd_words, wd_scales, us, wu_words, wu_scales, offs):
    idx = unstriped(offs)
    wdu = unpack_weight(wd_words, wd_scales, "e2m1")
    wuu = unpack_weight(wu_words, wu_scales, "e4m3")
    gidxq = mxq(f64(g)[:, idx], 0, "e5m2")
    dh = wdu.T @ gidxq
    m1 = dh.reshape(R, B, J // B).mean(axis=2)
    mr1 = np.repeat(m1, J // B, axis=1)
    dz = (0.5 * dh + 0.5 * mr1) * f64(us)
    dzq = mxq(dz, 0, "e5m2")
    y = wuu.T @ dzq
    return y

@@ -1,0 +1,166 @@
+from contextlib import ExitStack
+
+import concourse.mybir as mybir
+
+K, R, N, T, J = 512, 512, 512, 1024, 512
+FLOPS = 2 * N * R * J + 2 * R * K * J
+
+F32 = mybir.dt.float32
+BF16 = mybir.dt.bfloat16
+I32 = mybir.dt.int32
+U32 = mybir.dt.uint32
+U16 = mybir.dt.uint16
+U8 = mybir.dt.uint8
+E5M2 = mybir.dt.float8_e5m2_x4
+E4M3 = mybir.dt.float8_e4m3fn_x4
+E2M1 = mybir.dt.float4_e2m1fn_x4
+ADD = mybir.AluOpType.add
+MULT = mybir.AluOpType.mult
+
+P = 128
+PACK = 4
+GROUP = 4
+B = J // GROUP
+HALF = J // 2
+
+
+def load_scale_rows(queue, plane, scales):
+    for q in range(4):
+        queue.dma_start(out=plane[32 * q : 32 * q + 4, :].bitcast(I32), in_=scales[0, 4 * q : 4 * q + 4, :].bitcast(I32))
+
+
+def quantize_columns(nc, codes, plane, woven, c0, c1):
+    nc.vector.quantize_mx(
+        out=codes[:, c0:c1].bitcast(E5M2),
+        scales=plane[:, c0:c1],
+        in_=woven[:, c0:c1, :].rearrange("p j t -> p (j t)"),
+    )
+
+
+def tile_list_gradient_shared_in_groups_kernel(tc, g, wd_words, wd_scales, us, wu_words, wu_scales, offs, out):
+    nc = tc.nc
+    with ExitStack() as ctx:
+        sb = ctx.enter_context(tc.tile_pool(name="sb", bufs=1))
+        ps = ctx.enter_context(tc.psum_pool(name="ps", bufs=1))
+
+        offsets = sb.tile([P, J // 16], U16, name="offsets")
+        wd_raw = sb.tile([P, 2 * R], U8, name="wd_raw", align_bytes=64)
+        wd_plane_raw = sb.tile([P, R], U8, name="wd_plane_raw", align_bytes=64)
+        wd = sb.tile([P, 2 * R], U8, name="wd", align_bytes=64)
+        wd_plane = sb.tile([P, R], U8, name="wd_plane", align_bytes=64)
+        wu = sb.tile([P, K], U32, name="wu", align_bytes=64)
+        wu_plane = sb.tile([P, K], U8, name="wu_plane", align_bytes=64)
+        us_sb = sb.tile([P, PACK], F32, name="us_sb")
+        own = sb.tile([P, PACK], F32, name="own")
+        shared = sb.tile([P, PACK], F32, name="shared")
+        rows = [sb.tile([P, T], F32, name=f"rows{t}") for t in range(PACK)]
+        picked = [sb.tile([P, 2, J], BF16, name=f"picked{u}", align_bytes=64) for u in range(2)]
+        g_woven = sb.tile([P, J, PACK], BF16, name="g_woven", align_bytes=64)
+        g_codes = sb.tile([P, J], U32, name="g_codes", align_bytes=64)
+        g_plane = sb.tile([P, J], U8, name="g_plane", align_bytes=64)
+        sums = [sb.tile([P, B], F32, name=f"sums{t}") for t in range(PACK)]
+        means = [sb.tile([P, B], F32, name=f"means{t}") for t in range(PACK)]
+        dz = [sb.tile([P, 2, J], BF16, name=f"dz{u}", align_bytes=64) for u in range(2)]
+        dz_woven = sb.tile([P, J, PACK], BF16, name="dz_woven", align_bytes=64)
+        dz_codes = sb.tile([P, J], U32, name="dz_codes", align_bytes=64)
+        dz_plane = sb.tile([P, J], U8, name="dz_plane", align_bytes=64)
+        result = [sb.tile([P, J], F32, name=f"result{c}") for c in range(K // P)]
+        dh = [ps.tile([P, J], F32, name=f"dh{t}") for t in range(PACK)]
+        y = [ps.tile([P, J], F32, name=f"y{c}") for c in range(K // P)]
+
+        nc.vector.memset(wd_plane_raw[:].bitcast(I32), 0)
+        nc.vector.memset(wu_plane[:].bitcast(I32), 0)
+
+        g_rows = g.rearrange("(p t) w -> t p w", t=PACK)
+        nc.sync.dma_start(out=wd_raw[:].bitcast(I32), in_=wd_words[0].bitcast(I32))
+        nc.sync.dma_start(out=rows[0][:], in_=g_rows[0])
+        nc.sync.dma_start(offsets[:], offs)
+        load_scale_rows(nc.scalar, wd_plane_raw, wd_scales)
+        nc.gpsimd.dma_start(out=us_sb[:], in_=us.rearrange("(p t) o -> p (t o)", t=PACK))
+        for t in range(1, PACK):
+            nc.sync.dma_start(out=rows[t][:], in_=g_rows[t])
+        nc.sync.dma_start(out=wu[:].bitcast(I32), in_=wu_words[0].rearrange("p n t -> p (n t)").bitcast(I32))
+        load_scale_rows(nc.sync, wu_plane, wu_scales)
+
+        nc.gpsimd.tensor_scalar(own[:], us_sb[:], 0.5, 0.0, MULT, ADD)
+        nc.gpsimd.tensor_scalar(shared[:], us_sb[:], 0.5 / GROUP, 0.0, MULT, ADD)
+
+        nc.vector.tensor_copy(
+            out=wd[:].rearrange("p (t m b) -> p t m b", t=PACK, b=2),
+            in_=wd_raw[:].rearrange("p (m t b) -> p t m b", t=PACK, b=2),
+        )
+        nc.vector.tensor_copy(
+            out=wd_plane[:].rearrange("p (t m) -> p t m", t=PACK),
+            in_=wd_plane_raw[:].rearrange("p (m t) -> p t m", t=PACK),
+        )
+
+        for t in range(PACK - 1):
+            nc.vector.tensor_copy(picked[t // 2][:, t % 2, :], rows[t][:].indirect(offsets[:]))
+        nc.scalar.copy(g_woven[:, :, 0:2], picked[0][:].rearrange("p t j -> p j t"))
+        for h in range(2):
+            nc.vector.tensor_copy(
+                picked[1][:, 1, h * HALF : (h + 1) * HALF],
+                rows[PACK - 1][:].indirect(offsets[:, h * HALF // 16 : (h + 1) * HALF // 16]),
+            )
+        nc.scalar.copy(g_woven[:, :HALF, 2:4], picked[1][:, :, :HALF].rearrange("p t j -> p j t"))
+        nc.vector.tensor_copy(g_woven[:, HALF:, 2:4], picked[1][:, :, HALF:].rearrange("p t j -> p j t"))
+        quantize_columns(nc, g_codes, g_plane, g_woven, 0, HALF)
+        quantize_columns(nc, g_codes, g_plane, g_woven, HALF, J)
+
+        for t in range(PACK):
+            nc.tensor.matmul_mx(
+                out=dh[t][:],
+                lhsT=wd[:, 2 * P * t : 2 * P * (t + 1)].bitcast(E2M1),
+                lhsT_scale=wd_plane[:, P * t : P * (t + 1)],
+                rhs=g_codes[:].bitcast(E5M2),
+                rhs_scale=g_plane[:],
+                start=True,
+                stop=True,
+            )
+
+        def group_mean(t):
+            nc.vector.tensor_reduce(
+                out=sums[t][:], in_=dh[t][:].rearrange("p (b i) -> p b i", i=GROUP), axis=mybir.AxisListType.X, op=ADD
+            )
+            nc.gpsimd.tensor_scalar(means[t][:], sums[t][:], shared[:, t : t + 1], 0.0, MULT, ADD)
+
+        def mix(t, c0, c1):
+            nc.vector.scalar_tensor_tensor(
+                out=dz[t // 2][:, t % 2, c0:c1].rearrange("p (b i) -> p b i", i=GROUP),
+                in0=dh[t][:, c0:c1].rearrange("p (b i) -> p b i", i=GROUP),
+                scalar=own[:, t : t + 1],
+                in1=means[t][:, c0 // GROUP : c1 // GROUP].unsqueeze(2).to_broadcast([P, (c1 - c0) // GROUP, GROUP]),
+                op0=MULT,
+                op1=ADD,
+            )
+
+        group_mean(0)
+        group_mean(1)
+        mix(0, 0, J)
+        mix(1, 0, J)
+        group_mean(2)
+        group_mean(3)
+        nc.scalar.copy(dz_woven[:, :, 0:2], dz[0][:].rearrange("p t j -> p j t"))
+        mix(2, 0, J)
+        mix(3, 0, HALF)
+        mix(3, HALF, J)
+        nc.scalar.copy(dz_woven[:, :HALF, 2:4], dz[1][:, :, :HALF].rearrange("p t j -> p j t"))
+        nc.vector.tensor_copy(dz_woven[:, HALF:, 2:4], dz[1][:, :, HALF:].rearrange("p t j -> p j t"))
+        quantize_columns(nc, dz_codes, dz_plane, dz_woven, 0, HALF)
+        quantize_columns(nc, dz_codes, dz_plane, dz_woven, HALF, J)
+
+        for c in range(K // P):
+            nc.tensor.matmul_mx(
+                out=y[c][:],
+                lhsT=wu[:, P * c : P * (c + 1)].bitcast(E4M3),
+                lhsT_scale=wu_plane[:, P * c : P * (c + 1)],
+                rhs=dz_codes[:].bitcast(E5M2),
+                rhs_scale=dz_plane[:],
+                start=True,
+                stop=True,
+            )
+            if c % 2 == 0:
+                nc.scalar.copy(result[c][:], y[c][:])
+            else:
+                nc.vector.tensor_copy(result[c][:], y[c][:])
+            nc.sync.dma_start(out=out[P * c : P * (c + 1), :], in_=result[c][:])

@@ -22,6 +22,8 @@ PACK = 4
 GROUP = 4
 B = J // GROUP
 HALF = J // 2
+PARTS = ((0, HALF), (HALF, 3 * J // 4), (3 * J // 4, J))
+COPY = mybir.ActivationFunctionType.Copy
 
 
 def load_scale_rows(queue, plane, scales):
@@ -29,12 +31,15 @@ def load_scale_rows(queue, plane, scales):
         queue.dma_start(out=plane[32 * q : 32 * q + 4, :].bitcast(I32), in_=scales[0, 4 * q : 4 * q + 4, :].bitcast(I32))
 
 
-def quantize_columns(nc, codes, plane, woven, c0, c1):
+def quantize_half(nc, codes, plane, woven, h):
+    cols = slice(h * HALF, (h + 1) * HALF)
     nc.vector.quantize_mx(
-        out=codes[:, c0:c1].bitcast(E5M2),
-        scales=plane[:, c0:c1],
-        in_=woven[:, c0:c1, :].rearrange("p j t -> p (j t)"),
+        out=codes[:, cols].bitcast(E5M2), scales=plane[:, cols], in_=woven[h][:].rearrange("p j t -> p (j t)")
     )
+
+
+def weave_pair(copy, woven, u, pair):
+    copy(woven[:, :, 2 * u : 2 * u + 2], pair.rearrange("p t j -> p j t"))
 
 
 def tile_list_gradient_shared_in_groups_kernel(tc, g, wd_words, wd_scales, us, wu_words, wu_scales, offs, out):
@@ -54,17 +59,22 @@ def tile_list_gradient_shared_in_groups_kernel(tc, g, wd_words, wd_scales, us, w
         own = sb.tile([P, PACK], F32, name="own")
         shared = sb.tile([P, PACK], F32, name="shared")
         rows = [sb.tile([P, T], F32, name=f"rows{t}") for t in range(PACK)]
-        picked = [sb.tile([P, 2, J], BF16, name=f"picked{u}", align_bytes=64) for u in range(2)]
-        g_woven = sb.tile([P, J, PACK], BF16, name="g_woven", align_bytes=64)
+        picked01 = sb.tile([P, 2, J], BF16, name="picked01", align_bytes=64)
+        picked23 = [sb.tile([P, 2, HALF], BF16, name=f"picked23_{h}", align_bytes=64) for h in range(2)]
+        g_woven = [sb.tile([P, HALF, PACK], BF16, name=f"g_woven{h}", align_bytes=64) for h in range(2)]
         g_codes = sb.tile([P, J], U32, name="g_codes", align_bytes=64)
         g_plane = sb.tile([P, J], U8, name="g_plane", align_bytes=64)
-        sums = [sb.tile([P, B], F32, name=f"sums{t}") for t in range(PACK)]
+        sums = [sb.tile([P, B], F32, name=f"sums{t}") for t in range(2)]
+        upper = [sb.tile([P, 2, B], F32, name=f"upper{t}") for t in range(PACK)]
+        halves = [sb.tile([P, 2, B], F32, name=f"halves{t}") for t in range(PACK)]
         means = [sb.tile([P, B], F32, name=f"means{t}") for t in range(PACK)]
-        dz = [sb.tile([P, 2, J], BF16, name=f"dz{u}", align_bytes=64) for u in range(2)]
-        dz_woven = sb.tile([P, J, PACK], BF16, name="dz_woven", align_bytes=64)
+        dz01 = sb.tile([P, 2, J], BF16, name="dz01", align_bytes=64)
+        dz23 = [sb.tile([P, 2, c1 - c0], BF16, name=f"dz23_{c0}", align_bytes=64) for c0, c1 in PARTS]
+        dz_woven = [sb.tile([P, HALF, PACK], BF16, name=f"dz_woven{h}", align_bytes=64) for h in range(2)]
         dz_codes = sb.tile([P, J], U32, name="dz_codes", align_bytes=64)
         dz_plane = sb.tile([P, J], U8, name="dz_plane", align_bytes=64)
         result = [sb.tile([P, J], F32, name=f"result{c}") for c in range(K // P)]
+        first = sb.tile([P, HALF], F32, name="first")
         dh = [ps.tile([P, J], F32, name=f"dh{t}") for t in range(PACK)]
         y = [ps.tile([P, J], F32, name=f"y{c}") for c in range(K // P)]
 
@@ -75,10 +85,10 @@ def tile_list_gradient_shared_in_groups_kernel(tc, g, wd_words, wd_scales, us, w
         nc.sync.dma_start(out=wd_raw[:].bitcast(I32), in_=wd_words[0].bitcast(I32))
         nc.sync.dma_start(out=rows[0][:], in_=g_rows[0])
         nc.sync.dma_start(offsets[:], offs)
-        load_scale_rows(nc.scalar, wd_plane_raw, wd_scales)
         nc.gpsimd.dma_start(out=us_sb[:], in_=us.rearrange("(p t) o -> p (t o)", t=PACK))
         for t in range(1, PACK):
             nc.sync.dma_start(out=rows[t][:], in_=g_rows[t])
+        load_scale_rows(nc.sync, wd_plane_raw, wd_scales)
         nc.sync.dma_start(out=wu[:].bitcast(I32), in_=wu_words[0].rearrange("p n t -> p (n t)").bitcast(I32))
         load_scale_rows(nc.sync, wu_plane, wu_scales)
 
@@ -89,23 +99,23 @@ def tile_list_gradient_shared_in_groups_kernel(tc, g, wd_words, wd_scales, us, w
             out=wd[:].rearrange("p (t m b) -> p t m b", t=PACK, b=2),
             in_=wd_raw[:].rearrange("p (m t b) -> p t m b", t=PACK, b=2),
         )
+
+        for t in range(2):
+            nc.vector.tensor_copy(picked01[:, t, :], rows[t][:].indirect(offsets[:]))
+        for h in range(2):
+            weave_pair(nc.scalar.copy, g_woven[h][:], 0, picked01[:, :, h * HALF : (h + 1) * HALF])
+        for t in range(2, PACK):
+            for h in range(2):
+                half_list = offsets[:, h * HALF // 16 : (h + 1) * HALF // 16]
+                nc.vector.tensor_copy(picked23[h][:, t - 2, :], rows[t][:].indirect(half_list))
+        weave_pair(nc.scalar.copy, g_woven[0][:], 1, picked23[0][:])
         nc.vector.tensor_copy(
             out=wd_plane[:].rearrange("p (t m) -> p t m", t=PACK),
             in_=wd_plane_raw[:].rearrange("p (m t) -> p t m", t=PACK),
         )
-
-        for t in range(PACK - 1):
-            nc.vector.tensor_copy(picked[t // 2][:, t % 2, :], rows[t][:].indirect(offsets[:]))
-        nc.scalar.copy(g_woven[:, :, 0:2], picked[0][:].rearrange("p t j -> p j t"))
-        for h in range(2):
-            nc.vector.tensor_copy(
-                picked[1][:, 1, h * HALF : (h + 1) * HALF],
-                rows[PACK - 1][:].indirect(offsets[:, h * HALF // 16 : (h + 1) * HALF // 16]),
-            )
-        nc.scalar.copy(g_woven[:, :HALF, 2:4], picked[1][:, :, :HALF].rearrange("p t j -> p j t"))
-        nc.vector.tensor_copy(g_woven[:, HALF:, 2:4], picked[1][:, :, HALF:].rearrange("p t j -> p j t"))
-        quantize_columns(nc, g_codes, g_plane, g_woven, 0, HALF)
-        quantize_columns(nc, g_codes, g_plane, g_woven, HALF, J)
+        weave_pair(nc.vector.tensor_copy, g_woven[1][:], 1, picked23[1][:])
+        quantize_half(nc, g_codes, g_plane, g_woven, 0)
+        quantize_half(nc, g_codes, g_plane, g_woven, 1)
 
         for t in range(PACK):
             nc.tensor.matmul_mx(
@@ -118,15 +128,23 @@ def tile_list_gradient_shared_in_groups_kernel(tc, g, wd_words, wd_scales, us, w
                 stop=True,
             )
 
-        def group_mean(t):
+        def group_mean_direct(t):
             nc.vector.tensor_reduce(
                 out=sums[t][:], in_=dh[t][:].rearrange("p (b i) -> p b i", i=GROUP), axis=mybir.AxisListType.X, op=ADD
             )
             nc.gpsimd.tensor_scalar(means[t][:], sums[t][:], shared[:, t : t + 1], 0.0, MULT, ADD)
 
-        def mix(t, c0, c1):
+        def group_mean(t):
+            by_member = dh[t][:].rearrange("p (b i) -> p i b", i=GROUP)
+            nc.scalar.activation(upper[t][:], by_member[:, 2:4, :], COPY, scale=shared[:, t : t + 1])
             nc.vector.scalar_tensor_tensor(
-                out=dz[t // 2][:, t % 2, c0:c1].rearrange("p (b i) -> p b i", i=GROUP),
+                out=halves[t][:], in0=by_member[:, 0:2, :], scalar=shared[:, t : t + 1], in1=upper[t][:], op0=MULT, op1=ADD
+            )
+            nc.gpsimd.tensor_tensor(means[t][:], halves[t][:, 0, :], halves[t][:, 1, :], ADD)
+
+        def mix(dst, t, c0, c1):
+            nc.vector.scalar_tensor_tensor(
+                out=dst.rearrange("p (b i) -> p b i", i=GROUP),
                 in0=dh[t][:, c0:c1].rearrange("p (b i) -> p b i", i=GROUP),
                 scalar=own[:, t : t + 1],
                 in1=means[t][:, c0 // GROUP : c1 // GROUP].unsqueeze(2).to_broadcast([P, (c1 - c0) // GROUP, GROUP]),
@@ -134,20 +152,35 @@ def tile_list_gradient_shared_in_groups_kernel(tc, g, wd_words, wd_scales, us, w
                 op1=ADD,
             )
 
-        group_mean(0)
-        group_mean(1)
-        mix(0, 0, J)
-        mix(1, 0, J)
+        def gpsimd_copy(dst, src):
+            nc.gpsimd.tensor_scalar(dst, src, 1.0, 0.0, MULT, ADD)
+
+        group_mean_direct(0)
+        group_mean_direct(1)
+        mix(dz01[:, 0, :], 0, 0, J)
         group_mean(2)
         group_mean(3)
-        nc.scalar.copy(dz_woven[:, :, 0:2], dz[0][:].rearrange("p t j -> p j t"))
-        mix(2, 0, J)
-        mix(3, 0, HALF)
-        mix(3, HALF, J)
-        nc.scalar.copy(dz_woven[:, :HALF, 2:4], dz[1][:, :, :HALF].rearrange("p t j -> p j t"))
-        nc.vector.tensor_copy(dz_woven[:, HALF:, 2:4], dz[1][:, :, HALF:].rearrange("p t j -> p j t"))
-        quantize_columns(nc, dz_codes, dz_plane, dz_woven, 0, HALF)
-        quantize_columns(nc, dz_codes, dz_plane, dz_woven, HALF, J)
+        mix(dz01[:, 1, :], 1, 0, J)
+        for repeat in range(2):
+            nc.tensor.matmul_mx(
+                out=dh[1][:],
+                lhsT=wd[:, 2 * P : 4 * P].bitcast(E2M1),
+                lhsT_scale=wd_plane[:, P : 2 * P],
+                rhs=g_codes[:].bitcast(E5M2),
+                rhs_scale=g_plane[:],
+                start=True,
+                stop=True,
+            )
+        weave_pair(gpsimd_copy, dz_woven[0][:], 0, dz01[:, :, :HALF])
+        weave_pair(nc.scalar.copy, dz_woven[1][:], 0, dz01[:, :, HALF:])
+        for part in range(3):
+            for t in range(2, PACK):
+                mix(dz23[part][:, t - 2, :], t, *PARTS[part])
+        weave_pair(nc.scalar.copy, dz_woven[0][:], 1, dz23[0][:])
+        weave_pair(nc.vector.tensor_copy, dz_woven[1][:, : HALF // 2, :], 1, dz23[1][:])
+        weave_pair(nc.vector.tensor_copy, dz_woven[1][:, HALF // 2 :, :], 1, dz23[2][:])
+        quantize_half(nc, dz_codes, dz_plane, dz_woven, 0)
+        quantize_half(nc, dz_codes, dz_plane, dz_woven, 1)
 
         for c in range(K // P):
             nc.tensor.matmul_mx(
@@ -159,8 +192,12 @@ def tile_list_gradient_shared_in_groups_kernel(tc, g, wd_words, wd_scales, us, w
                 start=True,
                 stop=True,
             )
-            if c % 2 == 0:
-                nc.scalar.copy(result[c][:], y[c][:])
-            else:
-                nc.vector.tensor_copy(result[c][:], y[c][:])
+            copy_out = nc.scalar.copy if c % 2 == 0 else nc.vector.tensor_copy
+            if c == 0:
+                copy_out(first[:], y[c][:, :HALF])
+                nc.sync.dma_start(out=out[:P, :HALF], in_=first[:])
+                copy_out(result[c][:, HALF:], y[c][:, HALF:])
+                nc.sync.dma_start(out=out[:P, HALF:], in_=result[c][:, HALF:])
+                continue
+            copy_out(result[c][:], y[c][:])
             nc.sync.dma_start(out=out[P * c : P * (c + 1), :], in_=result[c][:])

@@ -16,30 +16,33 @@ E4M3 = mybir.dt.float8_e4m3fn_x4
 E2M1 = mybir.dt.float4_e2m1fn_x4
 ADD = mybir.AluOpType.add
 MULT = mybir.AluOpType.mult
-
-P = 128
-PACK = 4
-GROUP = 4
-B = J // GROUP
-HALF = J // 2
-PARTS = ((0, HALF), (HALF, 3 * J // 4), (3 * J // 4, J))
 COPY = mybir.ActivationFunctionType.Copy
 
-
-def load_scale_rows(queue, plane, scales):
-    for q in range(4):
-        queue.dma_start(out=plane[32 * q : 32 * q + 4, :].bitcast(I32), in_=scales[0, 4 * q : 4 * q + 4, :].bitcast(I32))
-
-
-def quantize_half(nc, codes, plane, woven, h):
-    cols = slice(h * HALF, (h + 1) * HALF)
-    nc.vector.quantize_mx(
-        out=codes[:, cols].bitcast(E5M2), scales=plane[:, cols], in_=woven[h][:].rearrange("p j t -> p (j t)")
-    )
+P = 128
+LANES = 4
+QUADRANTS = 4
+GROUP = 4
+B = J // GROUP
+PER_COLUMN = 16
+HALF = J // 2
+HALVES = (slice(0, HALF), slice(HALF, J))
+WARM_PASSES = 2
 
 
-def weave_pair(copy, woven, u, pair):
-    copy(woven[:, :, 2 * u : 2 * u + 2], pair.rearrange("p t j -> p j t"))
+def load_scale_rows(nc, tile, scales):
+    for quadrant in range(QUADRANTS):
+        nc.sync.dma_start(
+            out=tile[32 * quadrant : 32 * quadrant + 4, :].bitcast(I32),
+            in_=scales[0, 4 * quadrant : 4 * quadrant + 4, :].bitcast(I32),
+        )
+
+
+def weave_pair(copy, woven, first_lane, pair):
+    copy(woven[:, :, first_lane : first_lane + 2], pair.rearrange("p t j -> p j t"))
+
+
+def quantize(nc, words, scale_bytes, woven):
+    nc.vector.quantize_mx(out=words.bitcast(E5M2), scales=scale_bytes, in_=woven.rearrange("p j t -> p (j t)"))
 
 
 def tile_list_gradient_shared_in_groups_kernel(tc, g, wd_words, wd_scales, us, wu_words, wu_scales, offs, out):
@@ -48,106 +51,114 @@ def tile_list_gradient_shared_in_groups_kernel(tc, g, wd_words, wd_scales, us, w
         sb = ctx.enter_context(tc.tile_pool(name="sb", bufs=1))
         ps = ctx.enter_context(tc.psum_pool(name="ps", bufs=1))
 
-        offsets = sb.tile([P, J // 16], U16, name="offsets")
+        offsets = sb.tile([P, J // PER_COLUMN], U16, name="offsets")
         wd_raw = sb.tile([P, 2 * R], U8, name="wd_raw", align_bytes=64)
-        wd_plane_raw = sb.tile([P, R], U8, name="wd_plane_raw", align_bytes=64)
+        wd_scale_raw = sb.tile([P, R], U8, name="wd_scale_raw", align_bytes=64)
         wd = sb.tile([P, 2 * R], U8, name="wd", align_bytes=64)
-        wd_plane = sb.tile([P, R], U8, name="wd_plane", align_bytes=64)
+        wd_scale = sb.tile([P, R], U8, name="wd_scale", align_bytes=64)
         wu = sb.tile([P, K], U32, name="wu", align_bytes=64)
-        wu_plane = sb.tile([P, K], U8, name="wu_plane", align_bytes=64)
-        us_sb = sb.tile([P, PACK], F32, name="us_sb")
-        own = sb.tile([P, PACK], F32, name="own")
-        shared = sb.tile([P, PACK], F32, name="shared")
-        rows = [sb.tile([P, T], F32, name=f"rows{t}") for t in range(PACK)]
+        wu_scale = sb.tile([P, K], U8, name="wu_scale", align_bytes=64)
+        us_sb = sb.tile([P, LANES], F32, name="us_sb")
+        own_factor = sb.tile([P, LANES], F32, name="own_factor")
+        sum_factor = sb.tile([P, LANES], F32, name="sum_factor")
+        g_lane = [sb.tile([P, T], F32, name=f"g_lane{t}") for t in range(LANES)]
         picked01 = sb.tile([P, 2, J], BF16, name="picked01", align_bytes=64)
-        picked23 = [sb.tile([P, 2, HALF], BF16, name=f"picked23_{h}", align_bytes=64) for h in range(2)]
-        g_woven = [sb.tile([P, HALF, PACK], BF16, name=f"g_woven{h}", align_bytes=64) for h in range(2)]
-        g_codes = sb.tile([P, J], U32, name="g_codes", align_bytes=64)
-        g_plane = sb.tile([P, J], U8, name="g_plane", align_bytes=64)
-        sums = [sb.tile([P, B], F32, name=f"sums{t}") for t in range(2)]
-        upper = [sb.tile([P, 2, B], F32, name=f"upper{t}") for t in range(PACK)]
-        halves = [sb.tile([P, 2, B], F32, name=f"halves{t}") for t in range(PACK)]
-        means = [sb.tile([P, B], F32, name=f"means{t}") for t in range(PACK)]
+        picked23 = sb.tile([P, 2, J], BF16, name="picked23", align_bytes=64)
+        g_lane0_bf16 = sb.tile([P, T], BF16, name="g_lane0_bf16")
+        g_woven = sb.tile([P, J, LANES], BF16, name="g_woven", align_bytes=64)
+        g_words = sb.tile([P, J], U32, name="g_words", align_bytes=64)
+        g_scale = sb.tile([P, J], U8, name="g_scale", align_bytes=64)
+        group_sum = {t: sb.tile([P, B], F32, name=f"group_sum{t}") for t in (0, 1)}
+        upper = {t: sb.tile([P, 2, B], F32, name=f"upper{t}") for t in (2, 3)}
+        pair_sum = {t: sb.tile([P, 2, B], F32, name=f"pair_sum{t}") for t in (2, 3)}
+        shared = [sb.tile([P, B], F32, name=f"shared{t}") for t in range(LANES)]
         dz01 = sb.tile([P, 2, J], BF16, name="dz01", align_bytes=64)
-        dz23 = [sb.tile([P, 2, c1 - c0], BF16, name=f"dz23_{c0}", align_bytes=64) for c0, c1 in PARTS]
-        dz_woven = [sb.tile([P, HALF, PACK], BF16, name=f"dz_woven{h}", align_bytes=64) for h in range(2)]
-        dz_codes = sb.tile([P, J], U32, name="dz_codes", align_bytes=64)
-        dz_plane = sb.tile([P, J], U8, name="dz_plane", align_bytes=64)
+        dz23 = sb.tile([P, 2, J], BF16, name="dz23", align_bytes=64)
+        dz_woven = [sb.tile([P, HALF, LANES], BF16, name=f"dz_woven{h}", align_bytes=64) for h in range(2)]
+        dz_words = sb.tile([P, J], U32, name="dz_words", align_bytes=64)
+        dz_scale = sb.tile([P, J], U8, name="dz_scale", align_bytes=64)
         result = [sb.tile([P, J], F32, name=f"result{c}") for c in range(K // P)]
-        first = sb.tile([P, HALF], F32, name="first")
-        dh = [ps.tile([P, J], F32, name=f"dh{t}") for t in range(PACK)]
+        dh = [ps.tile([P, J], F32, name=f"dh{t}") for t in range(LANES)]
         y = [ps.tile([P, J], F32, name=f"y{c}") for c in range(K // P)]
 
-        nc.vector.memset(wd_plane_raw[:].bitcast(I32), 0)
-        nc.vector.memset(wu_plane[:].bitcast(I32), 0)
+        nc.vector.memset(wd_scale_raw[:].bitcast(I32), 0)
+        nc.vector.memset(wu_scale[:].bitcast(I32), 0)
 
-        g_rows = g.rearrange("(p t) w -> t p w", t=PACK)
+        g_by_lane = g.rearrange("(p t) w -> t p w", t=LANES)
+        nc.sync.dma_start(out=g_lane[0][:], in_=g_by_lane[0])
         nc.sync.dma_start(out=wd_raw[:].bitcast(I32), in_=wd_words[0].bitcast(I32))
-        nc.sync.dma_start(out=rows[0][:], in_=g_rows[0])
         nc.sync.dma_start(offsets[:], offs)
-        nc.gpsimd.dma_start(out=us_sb[:], in_=us.rearrange("(p t) o -> p (t o)", t=PACK))
-        for t in range(1, PACK):
-            nc.sync.dma_start(out=rows[t][:], in_=g_rows[t])
-        load_scale_rows(nc.sync, wd_plane_raw, wd_scales)
+        nc.gpsimd.dma_start(out=us_sb[:], in_=us.rearrange("(p t) o -> p (t o)", t=LANES))
+        for t in range(1, LANES):
+            nc.sync.dma_start(out=g_lane[t][:], in_=g_by_lane[t])
+        load_scale_rows(nc, wd_scale_raw, wd_scales)
         nc.sync.dma_start(out=wu[:].bitcast(I32), in_=wu_words[0].rearrange("p n t -> p (n t)").bitcast(I32))
-        load_scale_rows(nc.sync, wu_plane, wu_scales)
+        load_scale_rows(nc, wu_scale, wu_scales)
 
-        nc.gpsimd.tensor_scalar(own[:], us_sb[:], 0.5, 0.0, MULT, ADD)
-        nc.gpsimd.tensor_scalar(shared[:], us_sb[:], 0.5 / GROUP, 0.0, MULT, ADD)
+        nc.gpsimd.tensor_scalar(own_factor[:], us_sb[:], 0.5, 0.0, MULT, ADD)
+        nc.gpsimd.tensor_scalar(sum_factor[:], us_sb[:], 0.5 / GROUP, 0.0, MULT, ADD)
 
         nc.vector.tensor_copy(
-            out=wd[:].rearrange("p (t m b) -> p t m b", t=PACK, b=2),
-            in_=wd_raw[:].rearrange("p (m t b) -> p t m b", t=PACK, b=2),
+            out=wd[:].rearrange("p (t m b) -> p t m b", t=LANES, b=2),
+            in_=wd_raw[:].rearrange("p (m t b) -> p t m b", t=LANES, b=2),
         )
 
-        for t in range(2):
-            nc.vector.tensor_copy(picked01[:, t, :], rows[t][:].indirect(offsets[:]))
-        for h in range(2):
-            weave_pair(nc.scalar.copy, g_woven[h][:], 0, picked01[:, :, h * HALF : (h + 1) * HALF])
-        for t in range(2, PACK):
-            for h in range(2):
-                half_list = offsets[:, h * HALF // 16 : (h + 1) * HALF // 16]
-                nc.vector.tensor_copy(picked23[h][:, t - 2, :], rows[t][:].indirect(half_list))
-        weave_pair(nc.scalar.copy, g_woven[0][:], 1, picked23[0][:])
+        nc.scalar.activation(g_lane0_bf16[:], g_lane[0][:], COPY)
+        nc.scalar.activation(picked01[:, 0, :], g_lane0_bf16[:].indirect(offsets[:]), COPY)
+        nc.vector.tensor_copy(picked01[:, 1, :], g_lane[1][:].indirect(offsets[:]))
+        nc.vector.tensor_copy(picked23[:, 0, :], g_lane[2][:].indirect(offsets[:]))
+        weave_pair(nc.scalar.copy, g_woven[:], 0, picked01[:])
+        for half in HALVES:
+            half_list = offsets[:, half.start // PER_COLUMN : half.stop // PER_COLUMN]
+            nc.vector.tensor_copy(picked23[:, 1, half], g_lane[3][:].indirect(half_list))
+        weave_pair(nc.scalar.copy, g_woven[:, HALVES[0], :], 2, picked23[:, :, HALVES[0]])
         nc.vector.tensor_copy(
-            out=wd_plane[:].rearrange("p (t m) -> p t m", t=PACK),
-            in_=wd_plane_raw[:].rearrange("p (m t) -> p t m", t=PACK),
+            out=wd_scale[:].rearrange("p (t m) -> p t m", t=LANES),
+            in_=wd_scale_raw[:].rearrange("p (m t) -> p t m", t=LANES),
         )
-        weave_pair(nc.vector.tensor_copy, g_woven[1][:], 1, picked23[1][:])
-        quantize_half(nc, g_codes, g_plane, g_woven, 0)
-        quantize_half(nc, g_codes, g_plane, g_woven, 1)
+        weave_pair(nc.vector.tensor_copy, g_woven[:, HALVES[1], :], 2, picked23[:, :, HALVES[1]])
+        quantize(nc, g_words[:], g_scale[:], g_woven[:])
 
-        for t in range(PACK):
+        def first_product(t):
             nc.tensor.matmul_mx(
                 out=dh[t][:],
                 lhsT=wd[:, 2 * P * t : 2 * P * (t + 1)].bitcast(E2M1),
-                lhsT_scale=wd_plane[:, P * t : P * (t + 1)],
-                rhs=g_codes[:].bitcast(E5M2),
-                rhs_scale=g_plane[:],
+                lhsT_scale=wd_scale[:, P * t : P * (t + 1)],
+                rhs=g_words[:].bitcast(E5M2),
+                rhs_scale=g_scale[:],
                 start=True,
                 stop=True,
             )
 
-        def group_mean_direct(t):
+        def shared_by_reduce(t):
             nc.vector.tensor_reduce(
-                out=sums[t][:], in_=dh[t][:].rearrange("p (b i) -> p b i", i=GROUP), axis=mybir.AxisListType.X, op=ADD
+                out=group_sum[t][:],
+                in_=dh[t][:].rearrange("p (b i) -> p b i", i=GROUP),
+                axis=mybir.AxisListType.X,
+                op=ADD,
             )
-            nc.gpsimd.tensor_scalar(means[t][:], sums[t][:], shared[:, t : t + 1], 0.0, MULT, ADD)
+            nc.gpsimd.tensor_scalar(shared[t][:], group_sum[t][:], sum_factor[:, t : t + 1], 0.0, MULT, ADD)
 
-        def group_mean(t):
+        def shared_by_three_engines(t):
             by_member = dh[t][:].rearrange("p (b i) -> p i b", i=GROUP)
-            nc.scalar.activation(upper[t][:], by_member[:, 2:4, :], COPY, scale=shared[:, t : t + 1])
+            nc.scalar.activation(upper[t][:], by_member[:, 2:4, :], COPY, scale=sum_factor[:, t : t + 1])
             nc.vector.scalar_tensor_tensor(
-                out=halves[t][:], in0=by_member[:, 0:2, :], scalar=shared[:, t : t + 1], in1=upper[t][:], op0=MULT, op1=ADD
+                out=pair_sum[t][:],
+                in0=by_member[:, 0:2, :],
+                scalar=sum_factor[:, t : t + 1],
+                in1=upper[t][:],
+                op0=MULT,
+                op1=ADD,
             )
-            nc.gpsimd.tensor_tensor(means[t][:], halves[t][:, 0, :], halves[t][:, 1, :], ADD)
+            nc.gpsimd.tensor_tensor(shared[t][:], pair_sum[t][:, 0, :], pair_sum[t][:, 1, :], ADD)
 
-        def mix(dst, t, c0, c1):
+        def make_dz(dst, t, slots):
+            groups = slice(slots.start // GROUP, slots.stop // GROUP)
             nc.vector.scalar_tensor_tensor(
                 out=dst.rearrange("p (b i) -> p b i", i=GROUP),
-                in0=dh[t][:, c0:c1].rearrange("p (b i) -> p b i", i=GROUP),
-                scalar=own[:, t : t + 1],
-                in1=means[t][:, c0 // GROUP : c1 // GROUP].unsqueeze(2).to_broadcast([P, (c1 - c0) // GROUP, GROUP]),
+                in0=dh[t][:, slots].rearrange("p (b i) -> p b i", i=GROUP),
+                scalar=own_factor[:, t : t + 1],
+                in1=shared[t][:, groups].unsqueeze(2).to_broadcast([P, groups.stop - groups.start, GROUP]),
                 op0=MULT,
                 op1=ADD,
             )
@@ -155,49 +166,38 @@ def tile_list_gradient_shared_in_groups_kernel(tc, g, wd_words, wd_scales, us, w
         def gpsimd_copy(dst, src):
             nc.gpsimd.tensor_scalar(dst, src, 1.0, 0.0, MULT, ADD)
 
-        group_mean_direct(0)
-        group_mean_direct(1)
-        mix(dz01[:, 0, :], 0, 0, J)
-        group_mean(2)
-        group_mean(3)
-        mix(dz01[:, 1, :], 1, 0, J)
-        for repeat in range(2):
-            nc.tensor.matmul_mx(
-                out=dh[1][:],
-                lhsT=wd[:, 2 * P : 4 * P].bitcast(E2M1),
-                lhsT_scale=wd_plane[:, P : 2 * P],
-                rhs=g_codes[:].bitcast(E5M2),
-                rhs_scale=g_plane[:],
-                start=True,
-                stop=True,
-            )
-        weave_pair(gpsimd_copy, dz_woven[0][:], 0, dz01[:, :, :HALF])
-        weave_pair(nc.scalar.copy, dz_woven[1][:], 0, dz01[:, :, HALF:])
-        for part in range(3):
-            for t in range(2, PACK):
-                mix(dz23[part][:, t - 2, :], t, *PARTS[part])
-        weave_pair(nc.scalar.copy, dz_woven[0][:], 1, dz23[0][:])
-        weave_pair(nc.vector.tensor_copy, dz_woven[1][:, : HALF // 2, :], 1, dz23[1][:])
-        weave_pair(nc.vector.tensor_copy, dz_woven[1][:, HALF // 2 :, :], 1, dz23[2][:])
-        quantize_half(nc, dz_codes, dz_plane, dz_woven, 0)
-        quantize_half(nc, dz_codes, dz_plane, dz_woven, 1)
+        for t in range(LANES):
+            first_product(t)
+
+        shared_by_reduce(0)
+        shared_by_reduce(1)
+        make_dz(dz01[:, 0, :], 0, slice(0, J))
+        shared_by_three_engines(2)
+        shared_by_three_engines(3)
+        make_dz(dz01[:, 1, :], 1, slice(0, J))
+        for repeat in range(WARM_PASSES):
+            first_product(1)
+        weave_pair(gpsimd_copy, dz_woven[0][:], 0, dz01[:, :, HALVES[0]])
+        weave_pair(nc.scalar.copy, dz_woven[1][:], 0, dz01[:, :, HALVES[1]])
+        for half in HALVES:
+            for t in (2, 3):
+                make_dz(dz23[:, t - 2, half], t, half)
+        weave_pair(nc.scalar.copy, dz_woven[0][:], 2, dz23[:, :, HALVES[0]])
+        weave_pair(nc.vector.tensor_copy, dz_woven[1][:], 2, dz23[:, :, HALVES[1]])
+        for h, half in enumerate(HALVES):
+            quantize(nc, dz_words[:, half], dz_scale[:, half], dz_woven[h][:])
 
         for c in range(K // P):
             nc.tensor.matmul_mx(
                 out=y[c][:],
                 lhsT=wu[:, P * c : P * (c + 1)].bitcast(E4M3),
-                lhsT_scale=wu_plane[:, P * c : P * (c + 1)],
-                rhs=dz_codes[:].bitcast(E5M2),
-                rhs_scale=dz_plane[:],
+                lhsT_scale=wu_scale[:, P * c : P * (c + 1)],
+                rhs=dz_words[:].bitcast(E5M2),
+                rhs_scale=dz_scale[:],
                 start=True,
                 stop=True,
             )
             copy_out = nc.scalar.copy if c % 2 == 0 else nc.vector.tensor_copy
-            if c == 0:
-                copy_out(first[:], y[c][:, :HALF])
-                nc.sync.dma_start(out=out[:P, :HALF], in_=first[:])
-                copy_out(result[c][:, HALF:], y[c][:, HALF:])
-                nc.sync.dma_start(out=out[:P, HALF:], in_=result[c][:, HALF:])
-                continue
-            copy_out(result[c][:], y[c][:])
-            nc.sync.dma_start(out=out[P * c : P * (c + 1), :], in_=result[c][:])
+            for slots in HALVES if c == 0 else (slice(0, J),):
+                copy_out(result[c][:, slots], y[c][:, slots])
+                nc.sync.dma_start(out=out[P * c : P * (c + 1), slots], in_=result[c][:, slots])

@@ -86,22 +86,17 @@ def tile_list_gradient_shared_in_groups_kernel(tc, g, wd_words, wd_scales, us, w
 
         g_by_lane = g.rearrange("(p t) w -> t p w", t=LANES)
         nc.sync.dma_start(out=g_lane[0][:], in_=g_by_lane[0])
-        nc.sync.dma_start(out=wd_raw[:].bitcast(I32), in_=wd_words[0].bitcast(I32))
         nc.sync.dma_start(offsets[:], offs)
         nc.gpsimd.dma_start(out=us_sb[:], in_=us.rearrange("(p t) o -> p (t o)", t=LANES))
         for t in range(1, LANES):
             nc.sync.dma_start(out=g_lane[t][:], in_=g_by_lane[t])
         load_scale_rows(nc, wd_scale_raw, wd_scales)
+        nc.sync.dma_start(out=wd_raw[:].bitcast(I32), in_=wd_words[0].bitcast(I32))
         nc.sync.dma_start(out=wu[:].bitcast(I32), in_=wu_words[0].rearrange("p n t -> p (n t)").bitcast(I32))
         load_scale_rows(nc, wu_scale, wu_scales)
 
         nc.gpsimd.tensor_scalar(own_factor[:], us_sb[:], 0.5, 0.0, MULT, ADD)
         nc.gpsimd.tensor_scalar(sum_factor[:], us_sb[:], 0.5 / GROUP, 0.0, MULT, ADD)
-
-        nc.vector.tensor_copy(
-            out=wd[:].rearrange("p (t m b) -> p t m b", t=LANES, b=2),
-            in_=wd_raw[:].rearrange("p (m t b) -> p t m b", t=LANES, b=2),
-        )
 
         nc.scalar.activation(g_lane0_bf16[:], g_lane[0][:], COPY)
         nc.scalar.activation(picked01[:, 0, :], g_lane0_bf16[:].indirect(offsets[:]), COPY)
@@ -117,6 +112,10 @@ def tile_list_gradient_shared_in_groups_kernel(tc, g, wd_words, wd_scales, us, w
             in_=wd_scale_raw[:].rearrange("p (m t) -> p t m", t=LANES),
         )
         weave_pair(nc.vector.tensor_copy, g_woven[:, HALVES[1], :], 2, picked23[:, :, HALVES[1]])
+        nc.vector.tensor_copy(
+            out=wd[:].bitcast(U16).rearrange("p (t m) -> p t m", t=LANES),
+            in_=wd_raw[:].bitcast(U16).rearrange("p (m t) -> p t m", t=LANES),
+        )
         quantize(nc, g_words[:], g_scale[:], g_woven[:])
 
         def first_product(t):

from contextlib import ExitStack

import concourse.mybir as mybir

K, R, N, T, J = 512, 512, 512, 1024, 512
FLOPS = 2 * N * R * J + 2 * R * K * J

F32 = mybir.dt.float32
BF16 = mybir.dt.bfloat16
I32 = mybir.dt.int32
U32 = mybir.dt.uint32
U16 = mybir.dt.uint16
U8 = mybir.dt.uint8
E5M2 = mybir.dt.float8_e5m2_x4
E4M3 = mybir.dt.float8_e4m3fn_x4
E2M1 = mybir.dt.float4_e2m1fn_x4
ADD = mybir.AluOpType.add
MULT = mybir.AluOpType.mult
COPY = mybir.ActivationFunctionType.Copy

P = 128
LANES = 4
QUADRANTS = 4
GROUP = 4
B = J // GROUP
PER_COLUMN = 16
HALF = J // 2
HALVES = (slice(0, HALF), slice(HALF, J))
WARM_PASSES = 2


def load_scale_rows(nc, tile, scales):
    for quadrant in range(QUADRANTS):
        nc.sync.dma_start(
            out=tile[32 * quadrant : 32 * quadrant + 4, :].bitcast(I32),
            in_=scales[0, 4 * quadrant : 4 * quadrant + 4, :].bitcast(I32),
        )


def weave_pair(copy, woven, first_lane, pair):
    copy(woven[:, :, first_lane : first_lane + 2], pair.rearrange("p t j -> p j t"))


def quantize(nc, words, scale_bytes, woven):
    nc.vector.quantize_mx(out=words.bitcast(E5M2), scales=scale_bytes, in_=woven.rearrange("p j t -> p (j t)"))


def tile_list_gradient_shared_in_groups_kernel(tc, g, wd_words, wd_scales, us, wu_words, wu_scales, offs, out):
    nc = tc.nc
    with ExitStack() as ctx:
        sb = ctx.enter_context(tc.tile_pool(name="sb", bufs=1))
        ps = ctx.enter_context(tc.psum_pool(name="ps", bufs=1))

        offsets = sb.tile([P, J // PER_COLUMN], U16, name="offsets")
        wd_raw = sb.tile([P, 2 * R], U8, name="wd_raw", align_bytes=64)
        wd_scale_raw = sb.tile([P, R], U8, name="wd_scale_raw", align_bytes=64)
        wd = sb.tile([P, 2 * R], U8, name="wd", align_bytes=64)
        wd_scale = sb.tile([P, R], U8, name="wd_scale", align_bytes=64)
        wu = sb.tile([P, K], U32, name="wu", align_bytes=64)
        wu_scale = sb.tile([P, K], U8, name="wu_scale", align_bytes=64)
        us_sb = sb.tile([P, LANES], F32, name="us_sb")
        own_factor = sb.tile([P, LANES], F32, name="own_factor")
        sum_factor = sb.tile([P, LANES], F32, name="sum_factor")
        g_lane = [sb.tile([P, T], F32, name=f"g_lane{t}") for t in range(LANES)]
        picked01 = sb.tile([P, 2, J], BF16, name="picked01", align_bytes=64)
        picked23 = sb.tile([P, 2, J], BF16, name="picked23", align_bytes=64)
        g_lane0_bf16 = sb.tile([P, T], BF16, name="g_lane0_bf16")
        g_woven = sb.tile([P, J, LANES], BF16, name="g_woven", align_bytes=64)
        g_words = sb.tile([P, J], U32, name="g_words", align_bytes=64)
        g_scale = sb.tile([P, J], U8, name="g_scale", align_bytes=64)
        group_sum = {t: sb.tile([P, B], F32, name=f"group_sum{t}") for t in (0, 1)}
        upper = {t: sb.tile([P, 2, B], F32, name=f"upper{t}") for t in (2, 3)}
        pair_sum = {t: sb.tile([P, 2, B], F32, name=f"pair_sum{t}") for t in (2, 3)}
        shared = [sb.tile([P, B], F32, name=f"shared{t}") for t in range(LANES)]
        dz01 = sb.tile([P, 2, J], BF16, name="dz01", align_bytes=64)
        dz23 = sb.tile([P, 2, J], BF16, name="dz23", align_bytes=64)
        dz_woven = [sb.tile([P, HALF, LANES], BF16, name=f"dz_woven{h}", align_bytes=64) for h in range(2)]
        dz_words = sb.tile([P, J], U32, name="dz_words", align_bytes=64)
        dz_scale = sb.tile([P, J], U8, name="dz_scale", align_bytes=64)
        result = [sb.tile([P, J], F32, name=f"result{c}") for c in range(K // P)]
        dh = [ps.tile([P, J], F32, name=f"dh{t}") for t in range(LANES)]
        y = [ps.tile([P, J], F32, name=f"y{c}") for c in range(K // P)]

        nc.vector.memset(wd_scale_raw[:].bitcast(I32), 0)
        nc.vector.memset(wu_scale[:].bitcast(I32), 0)

        g_by_lane = g.rearrange("(p t) w -> t p w", t=LANES)
        nc.sync.dma_start(out=g_lane[0][:], in_=g_by_lane[0])
        nc.sync.dma_start(offsets[:], offs)
        nc.gpsimd.dma_start(out=us_sb[:], in_=us.rearrange("(p t) o -> p (t o)", t=LANES))
        for t in range(1, LANES):
            nc.sync.dma_start(out=g_lane[t][:], in_=g_by_lane[t])
        load_scale_rows(nc, wd_scale_raw, wd_scales)
        nc.sync.dma_start(out=wd_raw[:].bitcast(I32), in_=wd_words[0].bitcast(I32))
        nc.sync.dma_start(out=wu[:].bitcast(I32), in_=wu_words[0].rearrange("p n t -> p (n t)").bitcast(I32))
        load_scale_rows(nc, wu_scale, wu_scales)

        nc.gpsimd.tensor_scalar(own_factor[:], us_sb[:], 0.5, 0.0, MULT, ADD)
        nc.gpsimd.tensor_scalar(sum_factor[:], us_sb[:], 0.5 / GROUP, 0.0, MULT, ADD)

        nc.scalar.activation(g_lane0_bf16[:], g_lane[0][:], COPY)
        nc.scalar.activation(picked01[:, 0, :], g_lane0_bf16[:].indirect(offsets[:]), COPY)
        nc.vector.tensor_copy(picked01[:, 1, :], g_lane[1][:].indirect(offsets[:]))
        nc.vector.tensor_copy(picked23[:, 0, :], g_lane[2][:].indirect(offsets[:]))
        weave_pair(nc.scalar.copy, g_woven[:], 0, picked01[:])
        for half in HALVES:
            half_list = offsets[:, half.start // PER_COLUMN : half.stop // PER_COLUMN]
            nc.vector.tensor_copy(picked23[:, 1, half], g_lane[3][:].indirect(half_list))
        weave_pair(nc.scalar.copy, g_woven[:, HALVES[0], :], 2, picked23[:, :, HALVES[0]])
        nc.vector.tensor_copy(
            out=wd_scale[:].rearrange("p (t m) -> p t m", t=LANES),
            in_=wd_scale_raw[:].rearrange("p (m t) -> p t m", t=LANES),
        )
        weave_pair(nc.vector.tensor_copy, g_woven[:, HALVES[1], :], 2, picked23[:, :, HALVES[1]])
        nc.vector.tensor_copy(
            out=wd[:].bitcast(U16).rearrange("p (t m) -> p t m", t=LANES),
            in_=wd_raw[:].bitcast(U16).rearrange("p (m t) -> p t m", t=LANES),
        )
        quantize(nc, g_words[:], g_scale[:], g_woven[:])

        def first_product(t):
            nc.tensor.matmul_mx(
                out=dh[t][:],
                lhsT=wd[:, 2 * P * t : 2 * P * (t + 1)].bitcast(E2M1),
                lhsT_scale=wd_scale[:, P * t : P * (t + 1)],
                rhs=g_words[:].bitcast(E5M2),
                rhs_scale=g_scale[:],
                start=True,
                stop=True,
            )

        def shared_by_reduce(t):
            nc.vector.tensor_reduce(
                out=group_sum[t][:],
                in_=dh[t][:].rearrange("p (b i) -> p b i", i=GROUP),
                axis=mybir.AxisListType.X,
                op=ADD,
            )
            nc.gpsimd.tensor_scalar(shared[t][:], group_sum[t][:], sum_factor[:, t : t + 1], 0.0, MULT, ADD)

        def shared_by_three_engines(t):
            by_member = dh[t][:].rearrange("p (b i) -> p i b", i=GROUP)
            nc.scalar.activation(upper[t][:], by_member[:, 2:4, :], COPY, scale=sum_factor[:, t : t + 1])
            nc.vector.scalar_tensor_tensor(
                out=pair_sum[t][:],
                in0=by_member[:, 0:2, :],
                scalar=sum_factor[:, t : t + 1],
                in1=upper[t][:],
                op0=MULT,
                op1=ADD,
            )
            nc.gpsimd.tensor_tensor(shared[t][:], pair_sum[t][:, 0, :], pair_sum[t][:, 1, :], ADD)

        def make_dz(dst, t, slots):
            groups = slice(slots.start // GROUP, slots.stop // GROUP)
            nc.vector.scalar_tensor_tensor(
                out=dst.rearrange("p (b i) -> p b i", i=GROUP),
                in0=dh[t][:, slots].rearrange("p (b i) -> p b i", i=GROUP),
                scalar=own_factor[:, t : t + 1],
                in1=shared[t][:, groups].unsqueeze(2).to_broadcast([P, groups.stop - groups.start, GROUP]),
                op0=MULT,
                op1=ADD,
            )

        def gpsimd_copy(dst, src):
            nc.gpsimd.tensor_scalar(dst, src, 1.0, 0.0, MULT, ADD)

        for t in range(LANES):
            first_product(t)

        shared_by_reduce(0)
        shared_by_reduce(1)
        make_dz(dz01[:, 0, :], 0, slice(0, J))
        shared_by_three_engines(2)
        shared_by_three_engines(3)
        make_dz(dz01[:, 1, :], 1, slice(0, J))
        for repeat in range(WARM_PASSES):
            first_product(1)
        weave_pair(gpsimd_copy, dz_woven[0][:], 0, dz01[:, :, HALVES[0]])
        weave_pair(nc.scalar.copy, dz_woven[1][:], 0, dz01[:, :, HALVES[1]])
        for half in HALVES:
            for t in (2, 3):
                make_dz(dz23[:, t - 2, half], t, half)
        weave_pair(nc.scalar.copy, dz_woven[0][:], 2, dz23[:, :, HALVES[0]])
        weave_pair(nc.vector.tensor_copy, dz_woven[1][:], 2, dz23[:, :, HALVES[1]])
        for h, half in enumerate(HALVES):
            quantize(nc, dz_words[:, half], dz_scale[:, half], dz_woven[h][:])

        for c in range(K // P):
            nc.tensor.matmul_mx(
                out=y[c][:],
                lhsT=wu[:, P * c : P * (c + 1)].bitcast(E4M3),
                lhsT_scale=wu_scale[:, P * c : P * (c + 1)],
                rhs=dz_words[:].bitcast(E5M2),
                rhs_scale=dz_scale[:],
                start=True,
                stop=True,
            )
            copy_out = nc.scalar.copy if c % 2 == 0 else nc.vector.tensor_copy
            for slots in HALVES if c == 0 else (slice(0, J),):
                copy_out(result[c][:, slots], y[c][:, slots])
                nc.sync.dma_start(out=out[P * c : P * (c + 1), slots], in_=result[c][:, slots])
